import numpy as np
import ml_dtypes


def mxq(x, axis, fmt="e4m3"):
    dtype, down = {"e4m3": (ml_dtypes.float8_e4m3fn, 7), "e5m2": (ml_dtypes.float8_e5m2, 14)}[fmt]
    v = np.moveaxis(np.asarray(x, np.float32).astype(ml_dtypes.bfloat16).astype(np.float64), axis, -1)
    blocks = v.reshape(v.shape[:-1] + (-1, 32))
    amax = np.abs(blocks).max(-1, keepdims=True)
    byte = np.maximum(np.where(amax > 0, np.frexp(amax)[1] - 1 + 127, 0) - down, 1)
    scale = np.exp2(byte - 127.0)
    codes = (blocks / scale).astype(np.float32).astype(dtype).astype(np.float64)
    return np.moveaxis((codes * scale).reshape(v.shape), -1, axis)


WIDE = False


def mx_kscale(k):
    if not WIDE:
        return np.ones(k)
    levels = np.array([10, -10, 5, -5, 0])
    if k % 512:
        return np.exp2(np.random.permutation(np.resize(levels, k // 32))).repeat(32)
    a = np.empty((k // 512, 16))
    for p in range(k // 512):
        a[p, :8] = np.random.permutation(np.resize(levels, 8))
        for g in range(8):
            far = levels[np.abs(levels - a[p, g]) >= 10]
            a[p, g + 8] = far[np.random.randint(len(far))]
    return np.exp2(a.ravel()).repeat(32)


def f64(x):
    return np.asarray(x).astype(np.float64)


def striped(idx):
    return np.tile(idx.reshape(-1, 16).T, (8, 1)).astype(np.uint16)


def unstriped(offs):
    return offs[:16].T.reshape(-1).astype(np.int64)


def striped8(idx):
    return np.concatenate([x.reshape(-1, 16).T for x in idx]).astype(np.uint16)


def runs(offs, k):
    lists = np.stack([offs[16 * r : 16 * r + 16].T.reshape(-1) for r in range(8)]).astype(np.int64)
    return lists[np.arange(k) % 512 // 64]


def pack_weight(w):
    k, n = w.shape
    w = f64(np.asarray(w, np.float32).astype(ml_dtypes.bfloat16)).reshape(k // 32, 32, n)
    amax = np.abs(w).max(1)
    byte = np.clip(np.where(amax > 0, np.frexp(amax)[1] - 1 + 127 - 7, 1), 1, 254)
    scaled = (w * np.exp2(127.0 - byte)[:, None, :]).reshape(k, n).astype(np.float32)
    words = np.ascontiguousarray(scaled.reshape(k // 512, 128, 4, n).transpose(0, 1, 3, 2)).astype(ml_dtypes.float8_e4m3fn).view(np.uint8)
    return words, np.ascontiguousarray(byte.astype(np.uint8).reshape(k // 512, 16, n))


def unpack_weight(words, scales):
    g, p, n, _ = words.shape
    vals = np.ascontiguousarray(words).view(ml_dtypes.float8_e4m3fn).astype(np.float64) * np.repeat(np.exp2(scales.astype(np.float64) - 127.0), 8, axis=1)[..., None]
    return vals.transpose(0, 1, 3, 2).reshape(g * 512, n)


K, T, S, G, H = 512, 2048, 512, 2048, 512


def setup_inputs():
    n = np.random.standard_normal
    s = mx_kscale(K)[:, None]
    packed_xT = pack_weight(n((K, T)) * s)
    packed_dT = pack_weight(n((K, G)) / s)
    return {
        "x_words": packed_xT[0],
        "x_scales": packed_xT[1],
        "d_words": packed_dT[0],
        "d_scales": packed_dT[1],
        "gs": (np.random.uniform(0.5, 1.5, (K, 1)) * s).astype(np.float32),
        "offs": striped(np.random.permutation(T)[:S]),
        "k1": striped8(np.random.randint(0, G, (8, H))),
        "n1": striped8(np.stack([np.random.permutation(S) for _ in range(8)])),
        "n2": striped8(np.stack([np.random.permutation(S) for _ in range(8)])),
        "n3": striped8(np.stack([np.random.permutation(S) for _ in range(8)])),
        "n4": striped8(np.stack([np.random.permutation(S) for _ in range(8)])),
    }


def reference(x_words, x_scales, d_words, d_scales, gs, offs, k1, n1, n2, n3, n4):
    d_k1 = unpack_weight(d_words, d_scales)[np.arange(K)[:, None], runs(k1, K)]
    xq = unpack_weight(x_words, x_scales)[:, unstriped(offs)]
    h = 0.0625 * (d_k1.T @ xq)
    z = f64(gs) * ((np.tanh(h[np.arange(H)[:, None], runs(n1, H)] - h)) * (h[np.arange(H)[:, None], runs(n2, H)]))
    h2 = 0.0625 * ((d_k1.T @ mxq(z, 0, "e4m3")))
    return h2[np.arange(H)[:, None], runs(n3, H)] - (h2[np.arange(H)[:, None], runs(n4, H)])

@@ -1,0 +1,235 @@
+from contextlib import ExitStack
+
+import concourse.mybir as mybir
+
+K, T, S, G, H = 512, 2048, 512, 2048, 512
+FLOPS = 2 * 2 * K * H * S
+
+F32 = mybir.dt.float32
+BF16 = mybir.dt.bfloat16
+I32 = mybir.dt.int32
+U32 = mybir.dt.uint32
+U16 = mybir.dt.uint16
+U8 = mybir.dt.uint8
+FP8X4 = mybir.dt.float8_e4m3fn_x4
+ACT = mybir.ActivationFunctionType
+ALU = mybir.AluOpType
+
+P = 128
+PACK = 4
+SIXTEENTH = 0.0625
+HALF = S // 2
+PARTS = ((0, 256), (256, 384), (384, 512))
+
+
+def tile_picked_ringfdifgap_none_p_kernel(
+    tc, x_words, x_scales, d_words, d_scales, gs, offs, k1, n1, n2, n3, n4, out
+):
+    nc = tc.nc
+    with ExitStack() as ctx:
+        lists = ctx.enter_context(tc.tile_pool(name="lists", bufs=1))
+        keep = ctx.enter_context(tc.tile_pool(name="keep", bufs=1))
+        psum = ctx.enter_context(tc.psum_pool(name="psum", bufs=1))
+
+        def list_tile(name):
+            return lists.tile([P, S // 16], U16, name=name)
+
+        def entries(list_sb, a, b):
+            return list_sb[:, a // 16 : b // 16]
+
+        def bank(index, width):
+            return psum.tile([P, width], F32, name="bank%d" % index, tag="bank%d" % index)
+
+        k1_sb, offs_sb = list_tile("k1_sb"), list_tile("offs_sb")
+        n1_sb, n2_sb, n3_sb, n4_sb = list_tile("n1_sb"), list_tile("n2_sb"), list_tile("n3_sb"), list_tile("n4_sb")
+
+        d_scale_table = keep.tile([P, G], U8, align_bytes=64)
+        x_scale_table = keep.tile([P, T], U8, align_bytes=64)
+        d_word_table = keep.tile([P, G], I32, align_bytes=64)
+        x_word_table = keep.tile([P, T], I32, align_bytes=64)
+        gs_sb = keep.tile([P, PACK], F32)
+
+        nc.gpsimd.memset(d_scale_table[:].bitcast(I32), 0)
+        nc.vector.memset(x_scale_table[:].bitcast(I32), 0)
+        nc.sync.dma_start(k1_sb[:], k1)
+        nc.sync.dma_start(d_scale_table[0:P:8, :].bitcast(I32), d_scales[0].bitcast(I32))
+        nc.sync.dma_start(x_scale_table[0:P:8, :].bitcast(I32), x_scales[0].bitcast(I32))
+        nc.sync.dma_start(offs_sb[:], offs)
+        nc.sync.dma_start(n1_sb[:], n1)
+        nc.sync.dma_start(n2_sb[:], n2)
+        nc.sync.dma_start(d_word_table[:], d_words[0].rearrange("p n t -> p (n t)").bitcast(I32))
+        nc.sync.dma_start(x_word_table[:], x_words[0].rearrange("p n t -> p (n t)").bitcast(I32))
+        nc.sync.dma_start(gs_sb[:], gs.rearrange("(p t) o -> p (t o)", t=PACK))
+        nc.sync.dma_start(n4_sb[:], n4)
+        nc.sync.dma_start(n3_sb[:], n3)
+
+        rows = [keep.tile([P, 2 * S], F32, name="rows%d" % t) for t in range(PACK)]
+        for t in range(PACK):
+            nc.vector.memset(rows[t][:, S:], 0.0)
+
+        d_scales_picked = keep.tile([P, H], U8, align_bytes=64)
+        x_scales_picked = keep.tile([P, S], U8, align_bytes=64)
+        planes = keep.tile([P, H + S], U8, align_bytes=64)
+        d_scale_plane = planes[:, :H]
+        x_scale_plane = planes[:, H:]
+        nc.vector.tensor_copy(d_scales_picked[:], d_scale_table[:].indirect(k1_sb[:]))
+        nc.vector.tensor_copy(x_scales_picked[:], x_scale_table[:].indirect(offs_sb[:]))
+        nc.vector.tensor_copy(
+            d_scale_plane.rearrange("p (t m) -> p m t", t=PACK),
+            d_scales_picked[:].rearrange("p (m t) -> p m t", t=PACK),
+        )
+        nc.vector.tensor_copy(x_scale_plane.bitcast(I32), x_scales_picked[:].bitcast(I32))
+        for s in range(1, 4):
+            nc.scalar.dma_start(planes[s:P:32, :].bitcast(I32), planes[8 * s : P : 32, :].bitcast(I32))
+
+        d_words_picked = keep.tile([P, H], U32, align_bytes=64)
+        d_codes = keep.tile([P, H], U32, align_bytes=64)
+        nc.vector.tensor_copy(d_words_picked[:], d_word_table[:].bitcast(U32).indirect(k1_sb[:]))
+        nc.vector.tensor_copy(
+            d_codes[:].rearrange("p (t c i) -> p c t i", t=PACK, i=4),
+            d_words_picked[:].rearrange("p (c i t) -> p c t i", t=PACK, i=4),
+        )
+
+        x_codes = keep.tile([P, S], U32, align_bytes=64)
+
+        def product(acc, t, codes, scales, a, b):
+            nc.tensor.matmul_mx(
+                out=acc,
+                lhsT=d_codes[:, t * P : (t + 1) * P].bitcast(FP8X4),
+                lhsT_scale=d_scale_plane[:, t * P : (t + 1) * P],
+                rhs=codes[:, a:b].bitcast(FP8X4),
+                rhs_scale=scales[:, a:b],
+                start=True,
+                stop=True,
+            )
+
+        plain = [keep.tile([P, S], F32, name="plain%d" % t) for t in range(PACK)]
+        weighted = [keep.tile([P, S], F32, name="weighted%d" % t) for t in range(PACK)]
+        accs = {}
+
+        def first_product(index, t, a, b):
+            acc = bank(index, b - a)
+            product(acc[:], t, x_codes, x_scale_plane, a, b)
+            accs[(t, a)] = acc
+
+        def to_rows(t, a, b):
+            nc.scalar.activation(rows[t][:, a:b], accs[(t, a)][:], ACT.Copy, scale=SIXTEENTH)
+
+        def to_plain(t, a, b):
+            nc.scalar.activation(plain[t][:, a:b], accs[(t, a)][:], ACT.Copy, scale=SIXTEENTH)
+
+        def to_weighted(t, a, b):
+            nc.scalar.activation(weighted[t][:, a:b], accs[(t, a)][:], ACT.Copy, scale=gs_sb[:, t : t + 1])
+
+        for a in (0, HALF):
+            b = a + HALF
+            nc.vector.tensor_copy(x_codes[:, a:b], x_word_table[:].bitcast(U32).indirect(entries(offs_sb, a, b)))
+            first_product(a // HALF, 0, a, b)
+            to_rows(0, a, b)
+            to_plain(0, a, b)
+        for t in (1, 2, 3):
+            first_product(1 + t, t, 0, S)
+        to_rows(1, 0, S)
+        to_plain(1, 0, S)
+
+        gap = [keep.tile([P, S], F32, name="gap%d" % t) for t in range(PACK)]
+        bent = [keep.tile([P, S], F32, name="bent%d" % t) for t in range(PACK)]
+        z_part = [keep.tile([P, PACK, b - a], F32, name="z_part%d" % a) for a, b in PARTS]
+
+        def subtract(t, a, b):
+            nc.vector.tensor_tensor(
+                gap[t][:, a:b], rows[t][:].indirect(entries(n1_sb, a, b)), plain[t][:, a:b], ALU.subtract
+            )
+
+        def tanh(t):
+            nc.scalar.activation(bent[t][:], gap[t][:], ACT.Tanh)
+
+        def multiply(t, c):
+            a, b = PARTS[c]
+            nc.vector.tensor_tensor(
+                z_part[c][:, t, :], weighted[t][:].indirect(entries(n2_sb, a, b)), bent[t][:, a:b], ALU.mult
+            )
+
+        z_codes = keep.tile([P, S], U32, align_bytes=64)
+        z_scale_plane = keep.tile([P, S], U8, align_bytes=64)
+        woven = [keep.tile([P, (b - a) * PACK], BF16, align_bytes=64, name="woven%d" % a) for a, b in PARTS]
+
+        def weave_views(c):
+            return (
+                woven[c][:].rearrange("p (c i t) -> p c t i", t=PACK, i=4),
+                z_part[c][:].rearrange("p t (c i) -> p c t i", i=4),
+            )
+
+        def weave_on_scalar(c):
+            dst, src = weave_views(c)
+            nc.scalar.activation(dst, src, ACT.Copy, scale=SIXTEENTH)
+
+        def weave_on_vector(c):
+            dst, src = weave_views(c)
+            nc.vector.tensor_scalar(dst, src, SIXTEENTH, None, ALU.mult)
+
+        def quantise(c):
+            a, b = PARTS[c]
+            nc.vector.quantize_mx(out=z_codes[:, a:b].bitcast(FP8X4), scales=z_scale_plane[:, a:b], in_=woven[c][:])
+
+        def second_product(index, t, a, b):
+            acc = bank(index, b - a)
+            product(acc[:], t, z_codes, z_scale_plane, a, b)
+            nc.scalar.activation(rows[t][:, a:b], acc[:], ACT.Copy, scale=SIXTEENTH)
+
+        subtract(0, 0, HALF)
+        subtract(0, HALF, S)
+        to_weighted(0, 0, HALF)
+        to_weighted(0, HALF, S)
+        tanh(0)
+        subtract(1, 0, S)
+        to_rows(2, 0, S)
+        to_plain(2, 0, S)
+        for c in range(3):
+            multiply(0, c)
+        to_weighted(1, 0, S)
+        tanh(1)
+        subtract(2, 0, S)
+        to_rows(3, 0, S)
+        to_plain(3, 0, S)
+        for c in range(3):
+            multiply(1, c)
+        to_weighted(2, 0, S)
+        tanh(2)
+        subtract(3, 0, S)
+        to_weighted(3, 0, S)
+        tanh(3)
+        for c in range(3):
+            multiply(2, c)
+            multiply(3, c)
+            if c < 2:
+                weave_on_scalar(c)
+        quantise(0)
+        second_product(5, 0, *PARTS[0])
+        weave_on_vector(2)
+        quantise(1)
+        second_product(6, 0, *PARTS[1])
+        quantise(2)
+        second_product(7, 0, *PARTS[2])
+        for t in (1, 2, 3):
+            second_product(t - 1, t, 0, S)
+
+        out_rows = out.rearrange("(p t) s -> p t s", t=PACK)
+        minus = [keep.tile([P, S], F32, name="minus%d" % t) for t in range(PACK)]
+        result = [keep.tile([P, S], F32, name="result%d" % t) for t in range(PACK)]
+
+        def fetch(t):
+            nc.vector.tensor_copy(minus[t][:], rows[t][:].indirect(n4_sb[:]))
+
+        def finish(t, a, b):
+            nc.vector.tensor_tensor(
+                result[t][:, a:b], rows[t][:].indirect(entries(n3_sb, a, b)), minus[t][:, a:b], ALU.subtract
+            )
+            nc.sync.dma_start(out_rows[:, t, a:b], result[t][:, a:b])
+
+        fetch(0)
+        for t in range(PACK - 1):
+            fetch(t + 1)
+            finish(t, 0, S)
+        finish(PACK - 1, 0, HALF)
+        finish(PACK - 1, HALF, S)

@@ -44,7 +44,7 @@ def tile_picked_ringfdifgap_none_p_kernel(
         n1_sb, n2_sb, n3_sb, n4_sb = list_tile("n1_sb"), list_tile("n2_sb"), list_tile("n3_sb"), list_tile("n4_sb")
 
         d_scale_table = keep.tile([P, G], U8, align_bytes=64)
-        x_scale_table = keep.tile([P, T], U8, align_bytes=64)
+        x_scale_table = keep.tile([P, T], U8, align_bytes=64, tag="x_scale_slot")
         d_word_table = keep.tile([P, G], I32, align_bytes=64)
         x_word_table = keep.tile([P, T], I32, align_bytes=64)
         gs_sb = keep.tile([P, PACK], F32)
@@ -57,30 +57,31 @@ def tile_picked_ringfdifgap_none_p_kernel(
         nc.sync.dma_start(offs_sb[:], offs)
         nc.sync.dma_start(n1_sb[:], n1)
         nc.sync.dma_start(n2_sb[:], n2)
+        nc.sync.dma_start(n4_sb[:], n4)
         nc.sync.dma_start(d_word_table[:], d_words[0].rearrange("p n t -> p (n t)").bitcast(I32))
         nc.sync.dma_start(x_word_table[:], x_words[0].rearrange("p n t -> p (n t)").bitcast(I32))
         nc.sync.dma_start(gs_sb[:], gs.rearrange("(p t) o -> p (t o)", t=PACK))
-        nc.sync.dma_start(n4_sb[:], n4)
         nc.sync.dma_start(n3_sb[:], n3)
 
-        rows = [keep.tile([P, 2 * S], F32, name="rows%d" % t) for t in range(PACK)]
-        for t in range(PACK):
-            nc.vector.memset(rows[t][:, S:], 0.0)
+        first_rows = keep.tile([P, S], F32)
+        wide = [keep.tile([P, 2 * S], F32, name="wide%d" % t) for t in range(PACK)]
+        rows = [first_rows] + wide[: PACK - 1]
+        plain = [w[:, S:] for w in wide]
 
         d_scales_picked = keep.tile([P, H], U8, align_bytes=64)
         x_scales_picked = keep.tile([P, S], U8, align_bytes=64)
-        planes = keep.tile([P, H + S], U8, align_bytes=64)
-        d_scale_plane = planes[:, :H]
-        x_scale_plane = planes[:, H:]
         nc.vector.tensor_copy(d_scales_picked[:], d_scale_table[:].indirect(k1_sb[:]))
         nc.vector.tensor_copy(x_scales_picked[:], x_scale_table[:].indirect(offs_sb[:]))
+        planes = keep.tile([P, H + S], U8, align_bytes=64, tag="x_scale_slot")
+        d_scale_plane = planes[:, :H]
+        x_scale_plane = planes[:, H:]
         nc.vector.tensor_copy(
             d_scale_plane.rearrange("p (t m) -> p m t", t=PACK),
             d_scales_picked[:].rearrange("p (m t) -> p m t", t=PACK),
         )
         nc.vector.tensor_copy(x_scale_plane.bitcast(I32), x_scales_picked[:].bitcast(I32))
         for s in range(1, 4):
-            nc.scalar.dma_start(planes[s:P:32, :].bitcast(I32), planes[8 * s : P : 32, :].bitcast(I32))
+            nc.sync.dma_start(planes[s:P:32, :].bitcast(I32), planes[8 * s : P : 32, :].bitcast(I32))
 
         d_words_picked = keep.tile([P, H], U32, align_bytes=64)
         d_codes = keep.tile([P, H], U32, align_bytes=64)
@@ -103,7 +104,6 @@ def tile_picked_ringfdifgap_none_p_kernel(
                 stop=True,
             )
 
-        plain = [keep.tile([P, S], F32, name="plain%d" % t) for t in range(PACK)]
         weighted = [keep.tile([P, S], F32, name="weighted%d" % t) for t in range(PACK)]
         accs = {}
 
@@ -126,91 +126,84 @@ def tile_picked_ringfdifgap_none_p_kernel(
             nc.vector.tensor_copy(x_codes[:, a:b], x_word_table[:].bitcast(U32).indirect(entries(offs_sb, a, b)))
             first_product(a // HALF, 0, a, b)
             to_rows(0, a, b)
-            to_plain(0, a, b)
+        nc.vector.tensor_scalar(plain[0][:, :HALF], accs[(0, 0)][:], SIXTEENTH, None, ALU.mult)
+        to_plain(0, HALF, S)
         for t in (1, 2, 3):
             first_product(1 + t, t, 0, S)
         to_rows(1, 0, S)
         to_plain(1, 0, S)
 
-        gap = [keep.tile([P, S], F32, name="gap%d" % t) for t in range(PACK)]
-        bent = [keep.tile([P, S], F32, name="bent%d" % t) for t in range(PACK)]
-        z_part = [keep.tile([P, PACK, b - a], F32, name="z_part%d" % a) for a, b in PARTS]
+        gap = keep.tile([P, PACK, S], F32)
+        bent = keep.tile([P, PACK, S], F32)
+        z_half = [keep.tile([P, PACK, HALF], F32, name="z_half%d" % c) for c in range(2)]
 
         def subtract(t, a, b):
             nc.vector.tensor_tensor(
-                gap[t][:, a:b], rows[t][:].indirect(entries(n1_sb, a, b)), plain[t][:, a:b], ALU.subtract
+                gap[:, t, a:b], rows[t][:].indirect(entries(n1_sb, a, b)), plain[t][:, a:b], ALU.subtract
             )
 
-        def tanh(t):
-            nc.scalar.activation(bent[t][:], gap[t][:], ACT.Tanh)
+        def tanh(t0, t1, a, b):
+            nc.scalar.activation(bent[:, t0:t1, a:b], gap[:, t0:t1, a:b], ACT.Tanh)
 
-        def multiply(t, c):
-            a, b = PARTS[c]
+        def z_columns(a, b):
+            return z_half[a // HALF][:, :, a % HALF : a % HALF + b - a]
+
+        def multiply(t, a, b):
             nc.vector.tensor_tensor(
-                z_part[c][:, t, :], weighted[t][:].indirect(entries(n2_sb, a, b)), bent[t][:, a:b], ALU.mult
+                z_columns(a, b)[:, t, :], weighted[t][:].indirect(entries(n2_sb, a, b)), bent[:, t, a:b], ALU.mult
             )
 
         z_codes = keep.tile([P, S], U32, align_bytes=64)
         z_scale_plane = keep.tile([P, S], U8, align_bytes=64)
-        woven = [keep.tile([P, (b - a) * PACK], BF16, align_bytes=64, name="woven%d" % a) for a, b in PARTS]
+        woven = keep.tile([P, S * PACK], BF16, align_bytes=64)
 
-        def weave_views(c):
-            return (
-                woven[c][:].rearrange("p (c i t) -> p c t i", t=PACK, i=4),
-                z_part[c][:].rearrange("p t (c i) -> p c t i", i=4),
+        def weave(a, b):
+            nc.scalar.activation(
+                woven[:, PACK * a : PACK * b].rearrange("p (c i t) -> p c t i", t=PACK, i=4),
+                z_columns(a, b).rearrange("p t (c i) -> p c t i", i=4),
+                ACT.Copy,
+                scale=SIXTEENTH,
             )
 
-        def weave_on_scalar(c):
-            dst, src = weave_views(c)
-            nc.scalar.activation(dst, src, ACT.Copy, scale=SIXTEENTH)
-
-        def weave_on_vector(c):
-            dst, src = weave_views(c)
-            nc.vector.tensor_scalar(dst, src, SIXTEENTH, None, ALU.mult)
-
-        def quantise(c):
-            a, b = PARTS[c]
-            nc.vector.quantize_mx(out=z_codes[:, a:b].bitcast(FP8X4), scales=z_scale_plane[:, a:b], in_=woven[c][:])
+        def quantise(a, b):
+            nc.vector.quantize_mx(
+                out=z_codes[:, a:b].bitcast(FP8X4), scales=z_scale_plane[:, a:b], in_=woven[:, PACK * a : PACK * b]
+            )
 
         def second_product(index, t, a, b):
             acc = bank(index, b - a)
             product(acc[:], t, z_codes, z_scale_plane, a, b)
-            nc.scalar.activation(rows[t][:, a:b], acc[:], ACT.Copy, scale=SIXTEENTH)
+            nc.scalar.activation(wide[t][:, a:b], acc[:], ACT.Copy, scale=SIXTEENTH)
 
         subtract(0, 0, HALF)
         subtract(0, HALF, S)
         to_weighted(0, 0, HALF)
         to_weighted(0, HALF, S)
-        tanh(0)
+        tanh(0, 1, 0, S)
         subtract(1, 0, S)
         to_rows(2, 0, S)
         to_plain(2, 0, S)
-        for c in range(3):
-            multiply(0, c)
-        to_weighted(1, 0, S)
-        tanh(1)
-        subtract(2, 0, S)
+        multiply(0, 0, HALF)
+        multiply(0, HALF, S)
         to_rows(3, 0, S)
         to_plain(3, 0, S)
-        for c in range(3):
-            multiply(1, c)
-        to_weighted(2, 0, S)
-        tanh(2)
+        subtract(2, 0, S)
+        to_weighted(1, 0, S)
+        tanh(1, 2, 0, S)
         subtract(3, 0, S)
+        to_weighted(2, 0, S)
         to_weighted(3, 0, S)
-        tanh(3)
-        for c in range(3):
-            multiply(2, c)
-            multiply(3, c)
-            if c < 2:
-                weave_on_scalar(c)
-        quantise(0)
-        second_product(5, 0, *PARTS[0])
-        weave_on_vector(2)
-        quantise(1)
-        second_product(6, 0, *PARTS[1])
-        quantise(2)
-        second_product(7, 0, *PARTS[2])
+        multiply(1, 0, HALF)
+        multiply(1, HALF, S)
+        tanh(2, 4, 0, HALF)
+        tanh(2, 4, HALF, S)
+        for a in range(0, S, P):
+            multiply(2, a, a + P)
+            multiply(3, a, a + P)
+            weave(a, a + P)
+        for index, (a, b) in enumerate(PARTS):
+            quantise(a, b)
+            second_product(5 + index, 0, a, b)
         for t in (1, 2, 3):
             second_product(t - 1, t, 0, S)
 
@@ -218,18 +211,27 @@ def tile_picked_ringfdifgap_none_p_kernel(
         minus = [keep.tile([P, S], F32, name="minus%d" % t) for t in range(PACK)]
         result = [keep.tile([P, S], F32, name="result%d" % t) for t in range(PACK)]
 
-        def fetch(t):
-            nc.vector.tensor_copy(minus[t][:], rows[t][:].indirect(n4_sb[:]))
+        def fetch(t, a, b):
+            nc.vector.tensor_copy(minus[t][:, a:b], wide[t][:].indirect(entries(n4_sb, a, b)))
 
         def finish(t, a, b):
             nc.vector.tensor_tensor(
-                result[t][:, a:b], rows[t][:].indirect(entries(n3_sb, a, b)), minus[t][:, a:b], ALU.subtract
+                result[t][:, a:b], wide[t][:].indirect(entries(n3_sb, a, b)), minus[t][:, a:b], ALU.subtract
             )
+
+        def store(t, a, b):
             nc.sync.dma_start(out_rows[:, t, a:b], result[t][:, a:b])
 
-        fetch(0)
-        for t in range(PACK - 1):
-            fetch(t + 1)
+        fetch(0, 0, HALF)
+        fetch(0, HALF, S)
+        finish(0, 0, HALF)
+        finish(0, HALF, S)
+        store(0, 0, S)
+        fetch(1, 0, S)
+        for t in (1, 2):
+            fetch(t + 1, 0, S)
             finish(t, 0, S)
-        finish(PACK - 1, 0, HALF)
-        finish(PACK - 1, HALF, S)
+            store(t, 0, S)
+        for a in (0, HALF):
+            finish(3, a, a + HALF)
+            store(3, a, a + HALF)

@@ -50,7 +50,9 @@ def tile_picked_ringfdifgap_none_p_kernel(
         gs_sb = keep.tile([P, PACK], F32)
 
         nc.gpsimd.memset(d_scale_table[:].bitcast(I32), 0)
-        nc.vector.memset(x_scale_table[:].bitcast(I32), 0)
+        x_scale_words = x_scale_table[:].bitcast(I32)
+        nc.vector.memset(x_scale_words[:, : T // 8 + 1], 0)
+        nc.vector.memset(x_scale_words[:, T // 8 + 1 :], 0)
         nc.sync.dma_start(k1_sb[:], k1)
         nc.sync.dma_start(d_scale_table[0:P:8, :].bitcast(I32), d_scales[0].bitcast(I32))
         nc.sync.dma_start(x_scale_table[0:P:8, :].bitcast(I32), x_scales[0].bitcast(I32))
@@ -104,7 +106,7 @@ def tile_picked_ringfdifgap_none_p_kernel(
                 stop=True,
             )
 
-        weighted = [keep.tile([P, S], F32, name="weighted%d" % t) for t in range(PACK)]
+        weighted = [keep.tile([P, (2 if t < 2 else 1) * S], F32, name="weighted%d" % t) for t in range(PACK)]
         accs = {}
 
         def first_product(index, t, a, b):
@@ -124,33 +126,36 @@ def tile_picked_ringfdifgap_none_p_kernel(
         for a in (0, HALF):
             b = a + HALF
             nc.vector.tensor_copy(x_codes[:, a:b], x_word_table[:].bitcast(U32).indirect(entries(offs_sb, a, b)))
-            first_product(a // HALF, 0, a, b)
-            to_rows(0, a, b)
-        nc.vector.tensor_scalar(plain[0][:, :HALF], accs[(0, 0)][:], SIXTEENTH, None, ALU.mult)
-        to_plain(0, HALF, S)
-        for t in (1, 2, 3):
-            first_product(1 + t, t, 0, S)
-        to_rows(1, 0, S)
-        to_plain(1, 0, S)
+            for t in (0, 1):
+                first_product(2 * t + a // HALF, t, a, b)
+        for t in (0, 1):
+            to_rows(t, 0, HALF)
+            nc.vector.tensor_scalar(plain[t][:, :HALF], accs[(t, 0)][:], SIXTEENTH, None, ALU.mult)
+        for t in (0, 1):
+            to_rows(t, HALF, S)
+            to_plain(t, HALF, S)
+        for t in (2, 3):
+            first_product(2 + t, t, 0, S)
 
-        gap = keep.tile([P, PACK, S], F32)
+        late_gap = keep.tile([P, 2, S], F32)
+        gap = [weighted[0][:, S:], weighted[1][:, S:], late_gap[:, 0, :], late_gap[:, 1, :]]
         bent = keep.tile([P, PACK, S], F32)
-        z_half = [keep.tile([P, PACK, HALF], F32, name="z_half%d" % c) for c in range(2)]
+        z = keep.tile([P, PACK, S], F32)
 
         def subtract(t, a, b):
             nc.vector.tensor_tensor(
-                gap[:, t, a:b], rows[t][:].indirect(entries(n1_sb, a, b)), plain[t][:, a:b], ALU.subtract
+                gap[t][:, a:b], rows[t][:].indirect(entries(n1_sb, a, b)), plain[t][:, a:b], ALU.subtract
             )
 
-        def tanh(t0, t1, a, b):
-            nc.scalar.activation(bent[:, t0:t1, a:b], gap[:, t0:t1, a:b], ACT.Tanh)
+        def tanh(t):
+            nc.scalar.activation(bent[:, t, :], gap[t], ACT.Tanh)
 
-        def z_columns(a, b):
-            return z_half[a // HALF][:, :, a % HALF : a % HALF + b - a]
+        def late_tanh(a, b):
+            nc.scalar.activation(bent[:, 2:, a:b], late_gap[:, :, a:b], ACT.Tanh)
 
         def multiply(t, a, b):
             nc.vector.tensor_tensor(
-                z_columns(a, b)[:, t, :], weighted[t][:].indirect(entries(n2_sb, a, b)), bent[:, t, a:b], ALU.mult
+                z[:, t, a:b], weighted[t][:].indirect(entries(n2_sb, a, b)), bent[:, t, a:b], ALU.mult
             )
 
         z_codes = keep.tile([P, S], U32, align_bytes=64)
@@ -160,7 +165,7 @@ def tile_picked_ringfdifgap_none_p_kernel(
         def weave(a, b):
             nc.scalar.activation(
                 woven[:, PACK * a : PACK * b].rearrange("p (c i t) -> p c t i", t=PACK, i=4),
-                z_columns(a, b).rearrange("p t (c i) -> p c t i", i=4),
+                z[:, :, a:b].rearrange("p t (c i) -> p c t i", i=4),
                 ACT.Copy,
                 scale=SIXTEENTH,
             )
@@ -179,33 +184,32 @@ def tile_picked_ringfdifgap_none_p_kernel(
         subtract(0, HALF, S)
         to_weighted(0, 0, HALF)
         to_weighted(0, HALF, S)
-        tanh(0, 1, 0, S)
+        tanh(0)
         subtract(1, 0, S)
         to_rows(2, 0, S)
         to_plain(2, 0, S)
-        multiply(0, 0, HALF)
-        multiply(0, HALF, S)
+        multiply(0, 0, S)
         to_rows(3, 0, S)
         to_plain(3, 0, S)
         subtract(2, 0, S)
-        to_weighted(1, 0, S)
-        tanh(1, 2, 0, S)
+        to_weighted(1, 0, HALF)
+        to_weighted(1, HALF, S)
+        tanh(1)
         subtract(3, 0, S)
         to_weighted(2, 0, S)
         to_weighted(3, 0, S)
-        multiply(1, 0, HALF)
-        multiply(1, HALF, S)
-        tanh(2, 4, 0, HALF)
-        tanh(2, 4, HALF, S)
+        multiply(1, 0, S)
+        late_tanh(0, HALF)
+        late_tanh(HALF, S)
         for a in range(0, S, P):
             multiply(2, a, a + P)
             multiply(3, a, a + P)
             weave(a, a + P)
         for index, (a, b) in enumerate(PARTS):
             quantise(a, b)
-            second_product(5 + index, 0, a, b)
+            second_product((6 + index) % 8, 0, a, b)
         for t in (1, 2, 3):
-            second_product(t - 1, t, 0, S)
+            second_product(t, t, 0, S)
 
         out_rows = out.rearrange("(p t) s -> p t s", t=PACK)
         minus = [keep.tile([P, S], F32, name="minus%d" % t) for t in range(PACK)]

from contextlib import ExitStack

import concourse.mybir as mybir

K, T, S, G, H = 512, 2048, 512, 2048, 512
FLOPS = 2 * 2 * K * H * S

F32 = mybir.dt.float32
BF16 = mybir.dt.bfloat16
I32 = mybir.dt.int32
U32 = mybir.dt.uint32
U16 = mybir.dt.uint16
U8 = mybir.dt.uint8
FP8X4 = mybir.dt.float8_e4m3fn_x4
ACT = mybir.ActivationFunctionType
ALU = mybir.AluOpType

P = 128
PACK = 4
SIXTEENTH = 0.0625
HALF = S // 2
PARTS = ((0, 256), (256, 384), (384, 512))


def tile_picked_ringfdifgap_none_p_kernel(
    tc, x_words, x_scales, d_words, d_scales, gs, offs, k1, n1, n2, n3, n4, out
):
    nc = tc.nc
    with ExitStack() as ctx:
        lists = ctx.enter_context(tc.tile_pool(name="lists", bufs=1))
        keep = ctx.enter_context(tc.tile_pool(name="keep", bufs=1))
        psum = ctx.enter_context(tc.psum_pool(name="psum", bufs=1))

        def list_tile(name):
            return lists.tile([P, S // 16], U16, name=name)

        def entries(list_sb, a, b):
            return list_sb[:, a // 16 : b // 16]

        def bank(index, width):
            return psum.tile([P, width], F32, name="bank%d" % index, tag="bank%d" % index)

        k1_sb, offs_sb = list_tile("k1_sb"), list_tile("offs_sb")
        n1_sb, n2_sb, n3_sb, n4_sb = list_tile("n1_sb"), list_tile("n2_sb"), list_tile("n3_sb"), list_tile("n4_sb")

        d_scale_table = keep.tile([P, G], U8, align_bytes=64)
        x_scale_table = keep.tile([P, T], U8, align_bytes=64, tag="x_scale_slot")
        d_word_table = keep.tile([P, G], I32, align_bytes=64)
        x_word_table = keep.tile([P, T], I32, align_bytes=64)
        gs_sb = keep.tile([P, PACK], F32)

        nc.gpsimd.memset(d_scale_table[:].bitcast(I32), 0)
        x_scale_words = x_scale_table[:].bitcast(I32)
        nc.vector.memset(x_scale_words[:, : T // 8 + 1], 0)
        nc.vector.memset(x_scale_words[:, T // 8 + 1 :], 0)
        nc.sync.dma_start(k1_sb[:], k1)
        nc.sync.dma_start(d_scale_table[0:P:8, :].bitcast(I32), d_scales[0].bitcast(I32))
        nc.sync.dma_start(x_scale_table[0:P:8, :].bitcast(I32), x_scales[0].bitcast(I32))
        nc.sync.dma_start(offs_sb[:], offs)
        nc.sync.dma_start(n1_sb[:], n1)
        nc.sync.dma_start(n2_sb[:], n2)
        nc.sync.dma_start(n4_sb[:], n4)
        nc.sync.dma_start(d_word_table[:], d_words[0].rearrange("p n t -> p (n t)").bitcast(I32))
        nc.sync.dma_start(x_word_table[:], x_words[0].rearrange("p n t -> p (n t)").bitcast(I32))
        nc.sync.dma_start(gs_sb[:], gs.rearrange("(p t) o -> p (t o)", t=PACK))
        nc.sync.dma_start(n3_sb[:], n3)

        first_rows = keep.tile([P, S], F32)
        wide = [keep.tile([P, 2 * S], F32, name="wide%d" % t) for t in range(PACK)]
        rows = [first_rows] + wide[: PACK - 1]
        plain = [w[:, S:] for w in wide]

        d_scales_picked = keep.tile([P, H], U8, align_bytes=64)
        x_scales_picked = keep.tile([P, S], U8, align_bytes=64)
        nc.vector.tensor_copy(d_scales_picked[:], d_scale_table[:].indirect(k1_sb[:]))
        nc.vector.tensor_copy(x_scales_picked[:], x_scale_table[:].indirect(offs_sb[:]))
        planes = keep.tile([P, H + S], U8, align_bytes=64, tag="x_scale_slot")
        d_scale_plane = planes[:, :H]
        x_scale_plane = planes[:, H:]
        nc.vector.tensor_copy(
            d_scale_plane.rearrange("p (t m) -> p m t", t=PACK),
            d_scales_picked[:].rearrange("p (m t) -> p m t", t=PACK),
        )
        nc.vector.tensor_copy(x_scale_plane.bitcast(I32), x_scales_picked[:].bitcast(I32))
        for s in range(1, 4):
            nc.sync.dma_start(planes[s:P:32, :].bitcast(I32), planes[8 * s : P : 32, :].bitcast(I32))

        d_words_picked = keep.tile([P, H], U32, align_bytes=64)
        d_codes = keep.tile([P, H], U32, align_bytes=64)
        nc.vector.tensor_copy(d_words_picked[:], d_word_table[:].bitcast(U32).indirect(k1_sb[:]))
        nc.vector.tensor_copy(
            d_codes[:].rearrange("p (t c i) -> p c t i", t=PACK, i=4),
            d_words_picked[:].rearrange("p (c i t) -> p c t i", t=PACK, i=4),
        )

        x_codes = keep.tile([P, S], U32, align_bytes=64)

        def product(acc, t, codes, scales, a, b):
            nc.tensor.matmul_mx(
                out=acc,
                lhsT=d_codes[:, t * P : (t + 1) * P].bitcast(FP8X4),
                lhsT_scale=d_scale_plane[:, t * P : (t + 1) * P],
                rhs=codes[:, a:b].bitcast(FP8X4),
                rhs_scale=scales[:, a:b],
                start=True,
                stop=True,
            )

        weighted = [keep.tile([P, (2 if t < 2 else 1) * S], F32, name="weighted%d" % t) for t in range(PACK)]
        accs = {}

        def first_product(index, t, a, b):
            acc = bank(index, b - a)
            product(acc[:], t, x_codes, x_scale_plane, a, b)
            accs[(t, a)] = acc

        def to_rows(t, a, b):
            nc.scalar.activation(rows[t][:, a:b], accs[(t, a)][:], ACT.Copy, scale=SIXTEENTH)

        def to_plain(t, a, b):
            nc.scalar.activation(plain[t][:, a:b], accs[(t, a)][:], ACT.Copy, scale=SIXTEENTH)

        def to_weighted(t, a, b):
            nc.scalar.activation(weighted[t][:, a:b], accs[(t, a)][:], ACT.Copy, scale=gs_sb[:, t : t + 1])

        for a in (0, HALF):
            b = a + HALF
            nc.vector.tensor_copy(x_codes[:, a:b], x_word_table[:].bitcast(U32).indirect(entries(offs_sb, a, b)))
            for t in (0, 1):
                first_product(2 * t + a // HALF, t, a, b)
        for t in (0, 1):
            to_rows(t, 0, HALF)
            nc.vector.tensor_scalar(plain[t][:, :HALF], accs[(t, 0)][:], SIXTEENTH, None, ALU.mult)
        for t in (0, 1):
            to_rows(t, HALF, S)
            to_plain(t, HALF, S)
        for t in (2, 3):
            first_product(2 + t, t, 0, S)

        late_gap = keep.tile([P, 2, S], F32)
        gap = [weighted[0][:, S:], weighted[1][:, S:], late_gap[:, 0, :], late_gap[:, 1, :]]
        bent = keep.tile([P, PACK, S], F32)
        z = keep.tile([P, PACK, S], F32)

        def subtract(t, a, b):
            nc.vector.tensor_tensor(
                gap[t][:, a:b], rows[t][:].indirect(entries(n1_sb, a, b)), plain[t][:, a:b], ALU.subtract
            )

        def tanh(t):
            nc.scalar.activation(bent[:, t, :], gap[t], ACT.Tanh)

        def late_tanh(a, b):
            nc.scalar.activation(bent[:, 2:, a:b], late_gap[:, :, a:b], ACT.Tanh)

        def multiply(t, a, b):
            nc.vector.tensor_tensor(
                z[:, t, a:b], weighted[t][:].indirect(entries(n2_sb, a, b)), bent[:, t, a:b], ALU.mult
            )

        z_codes = keep.tile([P, S], U32, align_bytes=64)
        z_scale_plane = keep.tile([P, S], U8, align_bytes=64)
        woven = keep.tile([P, S * PACK], BF16, align_bytes=64)

        def weave(a, b):
            nc.scalar.activation(
                woven[:, PACK * a : PACK * b].rearrange("p (c i t) -> p c t i", t=PACK, i=4),
                z[:, :, a:b].rearrange("p t (c i) -> p c t i", i=4),
                ACT.Copy,
                scale=SIXTEENTH,
            )

        def quantise(a, b):
            nc.vector.quantize_mx(
                out=z_codes[:, a:b].bitcast(FP8X4), scales=z_scale_plane[:, a:b], in_=woven[:, PACK * a : PACK * b]
            )

        def second_product(index, t, a, b):
            acc = bank(index, b - a)
            product(acc[:], t, z_codes, z_scale_plane, a, b)
            nc.scalar.activation(wide[t][:, a:b], acc[:], ACT.Copy, scale=SIXTEENTH)

        subtract(0, 0, HALF)
        subtract(0, HALF, S)
        to_weighted(0, 0, HALF)
        to_weighted(0, HALF, S)
        tanh(0)
        subtract(1, 0, S)
        to_rows(2, 0, S)
        to_plain(2, 0, S)
        multiply(0, 0, S)
        to_rows(3, 0, S)
        to_plain(3, 0, S)
        subtract(2, 0, S)
        to_weighted(1, 0, HALF)
        to_weighted(1, HALF, S)
        tanh(1)
        subtract(3, 0, S)
        to_weighted(2, 0, S)
        to_weighted(3, 0, S)
        multiply(1, 0, S)
        late_tanh(0, HALF)
        late_tanh(HALF, S)
        for a in range(0, S, P):
            multiply(2, a, a + P)
            multiply(3, a, a + P)
            weave(a, a + P)
        for index, (a, b) in enumerate(PARTS):
            quantise(a, b)
            second_product((6 + index) % 8, 0, a, b)
        for t in (1, 2, 3):
            second_product(t, t, 0, S)

        out_rows = out.rearrange("(p t) s -> p t s", t=PACK)
        minus = [keep.tile([P, S], F32, name="minus%d" % t) for t in range(PACK)]
        result = [keep.tile([P, S], F32, name="result%d" % t) for t in range(PACK)]

        def fetch(t, a, b):
            nc.vector.tensor_copy(minus[t][:, a:b], wide[t][:].indirect(entries(n4_sb, a, b)))

        def finish(t, a, b):
            nc.vector.tensor_tensor(
                result[t][:, a:b], wide[t][:].indirect(entries(n3_sb, a, b)), minus[t][:, a:b], ALU.subtract
            )

        def store(t, a, b):
            nc.sync.dma_start(out_rows[:, t, a:b], result[t][:, a:b])

        fetch(0, 0, HALF)
        fetch(0, HALF, S)
        finish(0, 0, HALF)
        finish(0, HALF, S)
        store(0, 0, S)
        fetch(1, 0, S)
        for t in (1, 2):
            fetch(t + 1, 0, S)
            finish(t, 0, S)
            store(t, 0, S)
        for a in (0, HALF):
            finish(3, a, a + HALF)
            store(3, a, a + HALF)
